import numpy as np
import ml_dtypes


def mxq(x, axis, fmt="e4m3"):
    dtype, down = {"e4m3": (ml_dtypes.float8_e4m3fn, 7), "e5m2": (ml_dtypes.float8_e5m2, 14)}[fmt]
    v = np.moveaxis(np.asarray(x, np.float32).astype(ml_dtypes.bfloat16).astype(np.float64), axis, -1)
    blocks = v.reshape(v.shape[:-1] + (-1, 32))
    amax = np.abs(blocks).max(-1, keepdims=True)
    byte = np.maximum(np.where(amax > 0, np.frexp(amax)[1] - 1 + 127, 0) - down, 1)
    scale = np.exp2(byte - 127.0)
    codes = (blocks / scale).astype(np.float32).astype(dtype).astype(np.float64)
    return np.moveaxis((codes * scale).reshape(v.shape), -1, axis)


WIDE = False


def mx_kscale(k):
    if not WIDE:
        return np.ones(k)
    levels = np.array([10, -10, 5, -5, 0])
    if k % 512:
        return np.exp2(np.random.permutation(np.resize(levels, k // 32))).repeat(32)
    a = np.empty((k // 512, 16))
    for p in range(k // 512):
        a[p, :8] = np.random.permutation(np.resize(levels, 8))
        for g in range(8):
            far = levels[np.abs(levels - a[p, g]) >= 10]
            a[p, g + 8] = far[np.random.randint(len(far))]
    return np.exp2(a.ravel()).repeat(32)


def f64(x):
    return np.asarray(x).astype(np.float64)


E2M1 = np.array([0.0, 0.5, 1.0, 1.5, 2.0, 3.0, 4.0, 6.0, -0.0, -0.5, -1.0, -1.5, -2.0, -3.0, -4.0, -6.0])


def pack_weight(w, fmt):
    k, n = w.shape
    w = f64(np.asarray(w, np.float32).astype(ml_dtypes.bfloat16)).reshape(k // 32, 32, n)
    amax = np.abs(w).max(1)
    if fmt == "e4m3":
        byte = np.frexp(amax)[1] - 1 + 127 - 7
    else:
        mant, ex = np.frexp(amax / 6.0)
        byte = np.where(mant > 0.5, ex, ex - 1) + 127
    byte = np.clip(np.where(amax > 0, byte, 1), 1, 254)
    scaled = (w * np.exp2(127.0 - byte)[:, None, :]).reshape(k, n).astype(np.float32)
    by_word = np.ascontiguousarray(scaled.reshape(k // 512, 128, 4, n).transpose(0, 1, 3, 2))
    if fmt == "e4m3":
        words = by_word.astype(ml_dtypes.float8_e4m3fn).view(np.uint8)
    else:
        c = by_word.astype(ml_dtypes.float4_e2m1fn).view(np.uint8) & 0xF
        words = (c[..., 0::2] | (c[..., 1::2] << 4)).reshape(k // 512, 128, 2 * n)
    return np.ascontiguousarray(words), np.ascontiguousarray(byte.astype(np.uint8).reshape(k // 512, 16, n))


def unpack_weight(words, scales, fmt):
    g, _, n = scales.shape
    words = np.ascontiguousarray(words).reshape(g, 128, n, -1)
    if fmt == "e4m3":
        vals = words.view(ml_dtypes.float8_e4m3fn).astype(np.float64)
    else:
        nib = np.empty((g, 128, n, 4), np.uint8)
        nib[..., 0::2] = words & 0xF
        nib[..., 1::2] = words >> 4
        vals = E2M1[nib]
    vals = vals * np.repeat(np.exp2(scales.astype(np.float64) - 127.0), 8, axis=1)[..., None]
    return vals.transpose(0, 1, 3, 2).reshape(g * 512, n)


def silu(v):
    return v / (1.0 + np.exp(-v))


def bf(x):
    return np.asarray(x, np.float32).astype(ml_dtypes.bfloat16)


def planes(Y):
    r, m = Y.shape
    b = f64(bf(Y)).reshape(r // 32, 32, m)
    amax = np.abs(b).max(1)
    byte = np.clip(np.where(amax > 0, np.frexp(amax)[1] - 1 + 127 - 7, 1), 1, 254)
    codes = (b * np.exp2(127.0 - byte)[:, None, :]).reshape(r, m).astype(np.float32).astype(ml_dtypes.float8_e4m3fn).view(np.uint8)
    words = codes.reshape(r // 512, 128, 4, m).transpose(0, 1, 3, 2)
    return np.ascontiguousarray(words), np.ascontiguousarray(byte.astype(np.uint8).reshape(r // 512, 16, m))


K, L, S, U, T, N = 1024, 512, 512, 512, 1024, 512


def setup_inputs():
    n = np.random.standard_normal
    fk = mx_kscale(K)
    fl = mx_kscale(L)
    xap = pack_weight(n((K, S)) / fk[:, None], "e2m1")
    wap = pack_weight(n((K, N)) * 1 / np.sqrt(K) * fk[:, None], "e4m3")
    wbp = pack_weight(n((K, N)) * 1 / np.sqrt(K) * fk[:, None], "e2m1")
    cxp = pack_weight(n((L, T)) / fl[:, None], "e4m3")
    wcp = pack_weight(n((L, N)) * 1 / np.sqrt(L) * fl[:, None], "e2m1")
    return {
        "xa_words": xap[0],
        "xa_scales": xap[1],
        "wa_words": wap[0],
        "wa_scales": wap[1],
        "xb": (n((K, U)) / fk[:, None]).astype(np.float32),
        "wb_words": wbp[0],
        "wb_scales": wbp[1],
        "cx_words": cxp[0],
        "cx_scales": cxp[1],
        "wc_words": wcp[0],
        "wc_scales": wcp[1],
    }


def reference(xa_words, xa_scales, wa_words, wa_scales, xb, wb_words, wb_scales, cx_words, cx_scales, wc_words, wc_scales):
    xau = unpack_weight(xa_words, xa_scales, "e2m1")
    wau = unpack_weight(wa_words, wa_scales, "e4m3")
    wbu = unpack_weight(wb_words, wb_scales, "e2m1")
    cxu = unpack_weight(cx_words, cx_scales, "e4m3")
    wcu = unpack_weight(wc_words, wc_scales, "e2m1")
    za = wau.T @ xau
    xbq = mxq(f64(xb), 0, "e4m3")
    zb = wbu.T @ xbq
    z = np.concatenate([za, zb], axis=1)
    p = wcu.T @ cxu
    y = silu(z + p)
    words, scales = planes(y)
    return y, words, scales

@@ -1,0 +1,236 @@
+from contextlib import ExitStack
+
+import concourse.mybir as mybir
+
+F32 = mybir.dt.float32
+BF16 = mybir.dt.bfloat16
+I32 = mybir.dt.int32
+U32 = mybir.dt.uint32
+U8 = mybir.dt.uint8
+FP8X4 = mybir.dt.float8_e4m3fn_x4
+FP4X4 = mybir.dt.float4_e2m1fn_x4
+SILU = mybir.ActivationFunctionType.Silu
+
+P = 128
+PACK = 4
+NF = 512
+TB = 512
+HALF = 256
+FLOPS = 3 * 2 * 1024 * 512 * 512
+
+
+def tile_mix_two_batches_one_context_pl_kernel(
+    tc, xa_words, xa_scales, wa_words, wa_scales, xb, wb_words, wb_scales,
+    cx_words, cx_scales, wc_words, wc_scales, out_0, out_1, out_2,
+):
+    nc = tc.nc
+    with ExitStack() as ctx:
+        sb = ctx.enter_context(tc.tile_pool(name="sb", bufs=1))
+        ps = ctx.enter_context(tc.psum_pool(name="ps", bufs=1))
+        ctx.enter_context(tc.manual_schedule())
+
+        def tile(name, shape, dtype):
+            return sb.tile(shape, dtype, name=name, align_bytes=64)
+
+        wa_raw = [tile("wa_raw%d" % z, [P, NF], I32) for z in range(2)]
+        wa = [tile("wa%d" % z, [P, NF], I32) for z in range(2)]
+        wa_s_raw = tile("wa_s_raw", [P, 2, NF], U8)
+        wa_s = tile("wa_s", [P, 2, NF], U8)
+        wb_raw = tile("wb_raw", [P, 2, 2 * NF], U8)
+        wb = tile("wb", [P, 2, 2 * NF], U8)
+        wb_s_raw = tile("wb_s_raw", [P, 2, NF], U8)
+        wb_s = tile("wb_s", [P, 2, NF], U8)
+        wc_raw = tile("wc_raw", [P, 1, 2 * NF], U8)
+        wc = tile("wc", [P, 1, 2 * NF], U8)
+        wc_s_raw = tile("wc_s_raw", [P, 1, NF], U8)
+        wc_s = tile("wc_s", [P, 1, NF], U8)
+        xa = tile("xa", [P, 2, 2 * TB], U8)
+        xa_s = tile("xa_s", [P, 2, TB], U8)
+        cx = tile("cx", [P, 2 * TB], I32)
+        cx_s = tile("cx_s", [P, 1, 2 * TB], U8)
+        xb_raw = {(g, h): tile("xb_raw%d%d" % (g, h), [P, PACK, HALF], F32) for g in range(2) for h in range(2)}
+        xb_bf = {(g, h): tile("xb_bf%d%d" % (g, h), [P, HALF, PACK], BF16) for g in range(2) for h in range(2)}
+        xq = [tile("xq%d" % g, [P, TB], U32) for g in range(2)]
+        xq_s = [tile("xq_s%d" % g, [P, TB], U8) for g in range(2)]
+        y_a = tile("y_a", [P, PACK, TB], F32)
+        y_b = tile("y_b", [P, 2, PACK, HALF], F32)
+        ya_bf = tile("ya_bf", [P, TB, PACK], BF16)
+        yb_bf = [tile("yb_bf%d" % h, [P, HALF, PACK], BF16) for h in range(2)]
+        words_a = tile("words_a", [P, TB], U32)
+        words_b = [tile("words_b%d" % h, [P, HALF], U32) for h in range(2)]
+        y_s = tile("y_s", [P, 2 * TB], U8)
+        acc_a = [ps.tile([P, TB], F32, name="acc_a%d" % r) for r in range(PACK)]
+        acc_b = [ps.tile([P, TB], F32, name="acc_b%d" % r) for r in range(PACK)]
+
+        out_rows = out_0.rearrange("(p r) t -> p r t", r=PACK)
+        out_words = out_1[0].rearrange("p t i -> p (t i)").bitcast(I32)
+
+        def zero(eng, plane):
+            eng.memset(plane[:].rearrange("p z c -> p (z c)").bitcast(U32), 0)
+
+        def load_scales(eng, plane, dram):
+            for q in range(4):
+                eng.dma_start(
+                    out=plane[32 * q : 32 * q + 4].bitcast(I32),
+                    in_=dram[:, 4 * q : 4 * q + 4, :].rearrange("z r c -> r z c").bitcast(I32),
+                )
+
+        def load_fp4(dst, dram):
+            nc.sync.dma_start(out=dst[:].bitcast(I32), in_=dram.rearrange("z p c -> p z c").bitcast(I32))
+
+        def load_fp8(dst, dram):
+            nc.sync.dma_start(out=dst[:], in_=dram.rearrange("p c i -> p (c i)").bitcast(I32))
+
+        def load_xb(g, h):
+            rows = xb[512 * g : 512 * (g + 1), HALF * h : HALF * (h + 1)]
+            nc.sync.dma_start(out=xb_raw[g, h][:], in_=rows.rearrange("(p j) u -> p j u", j=PACK))
+
+        def deal_fp8(z):
+            nc.vector.tensor_copy(
+                out=wa[z][:].rearrange("p (r a b) -> p a r b", r=PACK, b=4),
+                in_=wa_raw[z][:].rearrange("p (a b r) -> p a r b", r=PACK, b=4),
+            )
+
+        def deal_fp4(dst, raw):
+            nc.vector.tensor_copy(
+                out=dst[:].rearrange("p z (r m b) -> p z r m b", r=PACK, b=2),
+                in_=raw[:].rearrange("p z (m r b) -> p z r m b", r=PACK, b=2),
+            )
+
+        def deal_scales(dst, raw):
+            nc.vector.tensor_copy(
+                out=dst[:].rearrange("p z (r m) -> p z r m", r=PACK),
+                in_=raw[:].rearrange("p z (m r) -> p z r m", r=PACK),
+            )
+
+        def interleave(copy, dst, src, c0, c1):
+            copy(
+                out=dst[:, c0:c1, :].rearrange("p (c i) j -> p c j i", i=4),
+                in_=src[:, :, c0:c1].rearrange("p j (c i) -> p c j i", i=4),
+            )
+
+        def quantize(words, scales, src):
+            nc.vector.quantize_mx(out=words.bitcast(FP8X4), scales=scales, in_=src[:].rearrange("p c j -> p (c j)"))
+
+        def quantize_xb(g, h):
+            cols = slice(HALF * h, HALF * (h + 1))
+            quantize(xq[g][:, cols], xq_s[g][:, cols], xb_bf[g, h])
+
+        def fp4_cols(w, z, r):
+            return w[:, z, 2 * P * r : 2 * P * (r + 1)].bitcast(FP4X4)
+
+        def pass_a(z, r, start):
+            nc.tensor.matmul_mx(
+                out=acc_a[r][:], lhsT=wa[z][:, P * r : P * (r + 1)].bitcast(FP8X4),
+                lhsT_scale=wa_s[:, z, P * r : P * (r + 1)],
+                rhs=xa[:, z, :].bitcast(FP4X4), rhs_scale=xa_s[:, z, :], start=start, stop=False,
+            )
+
+        def pass_b(g, r, stop):
+            nc.tensor.matmul_mx(
+                out=acc_b[r][:], lhsT=fp4_cols(wb, g, r), lhsT_scale=wb_s[:, g, P * r : P * (r + 1)],
+                rhs=xq[g][:].bitcast(FP8X4), rhs_scale=xq_s[g][:], start=False, stop=stop,
+            )
+
+        def pass_c(acc, t0, r, start, stop):
+            nc.tensor.matmul_mx(
+                out=acc[r][:], lhsT=fp4_cols(wc, 0, r), lhsT_scale=wc_s[:, 0, P * r : P * (r + 1)],
+                rhs=cx[:, t0 : t0 + TB].bitcast(FP8X4), rhs_scale=cx_s[:, 0, t0 : t0 + TB], start=start, stop=stop,
+            )
+
+        def silu_b(r, h):
+            nc.scalar.activation(out=y_b[:, h, r, :], in_=acc_b[r][:, HALF * h : HALF * (h + 1)], func=SILU)
+
+        def store_words(src, t0, width):
+            nc.sync.dma_start(out=out_words[:, t0 : t0 + width], in_=src[:].bitcast(I32))
+
+        vcopy = nc.vector.tensor_copy
+        scopy = nc.scalar.copy
+
+        for plane in (wa_s_raw, xa_s, cx_s):
+            zero(nc.vector, plane)
+        zero(nc.gpsimd, wc_s_raw)
+        load_scales(nc.gpsimd, wc_s_raw, wc_scales)
+        zero(nc.gpsimd, wb_s_raw)
+        load_scales(nc.gpsimd, wb_s_raw, wb_scales)
+
+        load_fp8(wa_raw[0], wa_words[0])
+        load_scales(nc.sync, wa_s_raw, wa_scales)
+        load_fp4(xa, xa_words)
+        load_fp8(wa_raw[1], wa_words[1])
+        load_fp8(cx, cx_words[0])
+        load_scales(nc.sync, xa_s, xa_scales)
+        load_fp4(wc_raw, wc_words)
+        load_fp4(wb_raw, wb_words)
+        load_xb(0, 0)
+        load_scales(nc.sync, cx_s, cx_scales)
+        load_xb(0, 1)
+        load_xb(1, 0)
+        load_xb(1, 1)
+
+        deal_fp8(0)
+        deal_scales(wa_s, wa_s_raw)
+        deal_fp8(1)
+        deal_fp4(wc, wc_raw)
+        deal_scales(wc_s, wc_s_raw)
+        deal_fp4(wb, wb_raw)
+
+        for r in range(3):
+            pass_a(0, r, True)
+            pass_a(1, r, False)
+        for r in range(3):
+            pass_c(acc_a, 0, r, False, True)
+        pass_a(0, 3, True)
+        pass_a(1, 3, False)
+        pass_c(acc_a, 0, 3, False, True)
+        for r in range(PACK):
+            nc.scalar.activation(out=y_a[:, r, :], in_=acc_a[r][:], func=SILU)
+            nc.sync.dma_start(out=out_rows[:, r, 0:TB], in_=y_a[:, r, :])
+        for r in range(PACK):
+            pass_c(acc_b, TB, r, True, False)
+
+        interleave(vcopy, xb_bf[0, 0], xb_raw[0, 0], 0, HALF)
+        quantize_xb(0, 0)
+        interleave(vcopy, xb_bf[0, 1], xb_raw[0, 1], 0, HALF)
+        deal_scales(wb_s, wb_s_raw)
+        quantize_xb(0, 1)
+        for r in range(PACK):
+            pass_b(0, r, False)
+        interleave(vcopy, xb_bf[1, 0], xb_raw[1, 0], 0, HALF)
+        interleave(scopy, xb_bf[1, 1], xb_raw[1, 1], 160, HALF)
+        interleave(vcopy, xb_bf[1, 1], xb_raw[1, 1], 0, 160)
+        quantize_xb(1, 0)
+        quantize_xb(1, 1)
+        for r in range(PACK):
+            pass_b(1, r, True)
+
+        interleave(scopy, ya_bf, y_a, 0, 128)
+        interleave(vcopy, ya_bf, y_a, 128, TB)
+        quantize(words_a[:], y_s[:, 0:TB], ya_bf)
+
+        for r in range(2):
+            nc.scalar.activation(
+                out=y_b[:, :, r, :], in_=acc_b[r][:].rearrange("p (h c) -> p h c", h=2), func=SILU
+            )
+            nc.sync.dma_start(
+                out=out_rows[:, r, TB : 2 * TB].rearrange("p (h c) -> p h c", h=2), in_=y_b[:, :, r, :]
+            )
+        store_words(words_a, 0, TB)
+        for h in range(2):
+            silu_b(2, h)
+            silu_b(3, h)
+            t0 = TB + HALF * h
+            nc.sync.dma_start(out=out_rows[:, 2:4, t0 : t0 + HALF], in_=y_b[:, h, 2:4, :])
+            if h == 0:
+                interleave(vcopy, yb_bf[0], y_b[:, 0], 0, HALF)
+        interleave(scopy, yb_bf[1], y_b[:, 1], 160, HALF)
+        interleave(vcopy, yb_bf[1], y_b[:, 1], 0, 160)
+        for h in range(2):
+            t0 = TB + HALF * h
+            quantize(words_b[h][:], y_s[:, t0 : t0 + HALF], yb_bf[h])
+            store_words(words_b[h], t0, HALF)
+        for q in range(4):
+            eng = nc.sync if q < 2 else nc.scalar
+            eng.dma_start(
+                out=out_2[0, 4 * q : 4 * q + 4, :].bitcast(I32), in_=y_s[32 * q : 32 * q + 4, :].bitcast(I32)
+            )

@@ -32,22 +32,28 @@ def tile_mix_two_batches_one_context_pl_kernel(
         def tile(name, shape, dtype):
             return sb.tile(shape, dtype, name=name, align_bytes=64)
 
-        wa_raw = [tile("wa_raw%d" % z, [P, NF], I32) for z in range(2)]
+        wa_raw = tile("wa_raw", [P, 2, NF], I32)
         wa = [tile("wa%d" % z, [P, NF], I32) for z in range(2)]
-        wa_s_raw = tile("wa_s_raw", [P, 2, NF], U8)
+        staged = tile("staged", [16, 9 * NF], U8)
+        planes = tile("planes", [P, 9 * NF], U8)
+
+        def plane(first, passes, width):
+            return planes[:, first * NF : first * NF + passes * width].rearrange("p (z c) -> p z c", z=passes)
+
+        wc_s_raw = plane(0, 1, NF)
+        cx_s = plane(1, 1, 2 * TB)
+        wa_s_raw = plane(3, 2, NF)
+        xa_s = plane(5, 2, TB)
+        wb_s_raw = plane(7, 2, NF)
         wa_s = tile("wa_s", [P, 2, NF], U8)
         wb_raw = tile("wb_raw", [P, 2, 2 * NF], U8)
         wb = tile("wb", [P, 2, 2 * NF], U8)
-        wb_s_raw = tile("wb_s_raw", [P, 2, NF], U8)
         wb_s = tile("wb_s", [P, 2, NF], U8)
         wc_raw = tile("wc_raw", [P, 1, 2 * NF], U8)
         wc = tile("wc", [P, 1, 2 * NF], U8)
-        wc_s_raw = tile("wc_s_raw", [P, 1, NF], U8)
         wc_s = tile("wc_s", [P, 1, NF], U8)
         xa = tile("xa", [P, 2, 2 * TB], U8)
-        xa_s = tile("xa_s", [P, 2, TB], U8)
         cx = tile("cx", [P, 2 * TB], I32)
-        cx_s = tile("cx_s", [P, 1, 2 * TB], U8)
         xb_raw = {(g, h): tile("xb_raw%d%d" % (g, h), [P, PACK, HALF], F32) for g in range(2) for h in range(2)}
         xb_bf = {(g, h): tile("xb_bf%d%d" % (g, h), [P, HALF, PACK], BF16) for g in range(2) for h in range(2)}
         xq = [tile("xq%d" % g, [P, TB], U32) for g in range(2)]
@@ -65,15 +71,10 @@ def tile_mix_two_batches_one_context_pl_kernel(
         out_rows = out_0.rearrange("(p r) t -> p r t", r=PACK)
         out_words = out_1[0].rearrange("p t i -> p (t i)").bitcast(I32)
 
-        def zero(eng, plane):
-            eng.memset(plane[:].rearrange("p z c -> p (z c)").bitcast(U32), 0)
-
-        def load_scales(eng, plane, dram):
-            for q in range(4):
-                eng.dma_start(
-                    out=plane[32 * q : 32 * q + 4].bitcast(I32),
-                    in_=dram[:, 4 * q : 4 * q + 4, :].rearrange("z r c -> r z c").bitcast(I32),
-                )
+        def stage_scales(queue, first, dram):
+            passes, rows, width = dram.shape
+            dst = staged[:, first * NF : first * NF + passes * width].rearrange("q (z c) -> q z c", z=passes)
+            queue.dma_start(out=dst.bitcast(I32), in_=dram.rearrange("z q c -> q z c").bitcast(I32))
 
         def load_fp4(dst, dram):
             nc.sync.dma_start(out=dst[:].bitcast(I32), in_=dram.rearrange("z p c -> p z c").bitcast(I32))
@@ -88,19 +89,19 @@ def tile_mix_two_batches_one_context_pl_kernel(
         def deal_fp8(z):
             nc.vector.tensor_copy(
                 out=wa[z][:].rearrange("p (r a b) -> p a r b", r=PACK, b=4),
-                in_=wa_raw[z][:].rearrange("p (a b r) -> p a r b", r=PACK, b=4),
+                in_=wa_raw[:, z, :].rearrange("p (a b r) -> p a r b", r=PACK, b=4),
             )
 
-        def deal_fp4(dst, raw):
+        def deal_fp4(dst, raw, z):
             nc.vector.tensor_copy(
-                out=dst[:].rearrange("p z (r m b) -> p z r m b", r=PACK, b=2),
-                in_=raw[:].rearrange("p z (m r b) -> p z r m b", r=PACK, b=2),
+                out=dst[:, z, :].rearrange("p (r m b) -> p r m b", r=PACK, b=2),
+                in_=raw[:, z, :].rearrange("p (m r b) -> p r m b", r=PACK, b=2),
             )
 
         def deal_scales(dst, raw):
             nc.vector.tensor_copy(
                 out=dst[:].rearrange("p z (r m) -> p z r m", r=PACK),
-                in_=raw[:].rearrange("p z (m r) -> p z r m", r=PACK),
+                in_=raw.rearrange("p z (m r) -> p z r m", r=PACK),
             )
 
         def interleave(copy, dst, src, c0, c1):
@@ -119,11 +120,11 @@ def tile_mix_two_batches_one_context_pl_kernel(
         def fp4_cols(w, z, r):
             return w[:, z, 2 * P * r : 2 * P * (r + 1)].bitcast(FP4X4)
 
-        def pass_a(z, r, start):
+        def pass_a(z, r, stop):
             nc.tensor.matmul_mx(
                 out=acc_a[r][:], lhsT=wa[z][:, P * r : P * (r + 1)].bitcast(FP8X4),
                 lhsT_scale=wa_s[:, z, P * r : P * (r + 1)],
-                rhs=xa[:, z, :].bitcast(FP4X4), rhs_scale=xa_s[:, z, :], start=start, stop=False,
+                rhs=xa[:, z, :].bitcast(FP4X4), rhs_scale=xa_s[:, z, :], start=False, stop=stop,
             )
 
         def pass_b(g, r, stop):
@@ -147,84 +148,74 @@ def tile_mix_two_batches_one_context_pl_kernel(
         vcopy = nc.vector.tensor_copy
         scopy = nc.scalar.copy
 
-        for plane in (wa_s_raw, xa_s, cx_s):
-            zero(nc.vector, plane)
-        zero(nc.gpsimd, wc_s_raw)
-        load_scales(nc.gpsimd, wc_s_raw, wc_scales)
-        zero(nc.gpsimd, wb_s_raw)
-        load_scales(nc.gpsimd, wb_s_raw, wb_scales)
-
-        load_fp8(wa_raw[0], wa_words[0])
-        load_scales(nc.sync, wa_s_raw, wa_scales)
-        load_fp4(xa, xa_words)
-        load_fp8(wa_raw[1], wa_words[1])
-        load_fp8(cx, cx_words[0])
-        load_scales(nc.sync, xa_s, xa_scales)
+        nc.vector.memset(planes[:].bitcast(U32), 0)
+        stage_scales(nc.sync, 0, wc_scales)
+        stage_scales(nc.scalar, 1, cx_scales)
+        stage_scales(nc.sync, 3, wa_scales)
+        stage_scales(nc.scalar, 5, xa_scales)
+        stage_scales(nc.sync, 7, wb_scales)
         load_fp4(wc_raw, wc_words)
+        load_fp8(cx, cx_words[0])
+        nc.sync.dma_start(out=wa_raw[:], in_=wa_words.rearrange("z p c i -> p z (c i)").bitcast(I32))
+        for q in range(4):
+            nc.sync.dma_start(
+                out=planes[32 * q : 32 * q + 4, :].bitcast(I32), in_=staged[4 * q : 4 * q + 4, :].bitcast(I32)
+            )
         load_fp4(wb_raw, wb_words)
-        load_xb(0, 0)
-        load_scales(nc.sync, cx_s, cx_scales)
-        load_xb(0, 1)
-        load_xb(1, 0)
-        load_xb(1, 1)
+        load_fp4(xa, xa_words)
+        for g in range(2):
+            for h in range(2):
+                load_xb(g, h)
 
+        deal_fp4(wc, wc_raw, 0)
         deal_fp8(0)
-        deal_scales(wa_s, wa_s_raw)
         deal_fp8(1)
-        deal_fp4(wc, wc_raw)
+        deal_fp4(wb, wb_raw, 0)
         deal_scales(wc_s, wc_s_raw)
-        deal_fp4(wb, wb_raw)
+        deal_scales(wa_s, wa_s_raw)
+        deal_fp4(wb, wb_raw, 1)
+        deal_scales(wb_s, wb_s_raw)
 
-        for r in range(3):
-            pass_a(0, r, True)
-            pass_a(1, r, False)
-        for r in range(3):
-            pass_c(acc_a, 0, r, False, True)
-        pass_a(0, 3, True)
-        pass_a(1, 3, False)
-        pass_c(acc_a, 0, 3, False, True)
+        for r in range(PACK):
+            pass_c(acc_a, 0, r, True, False)
+        for r in range(PACK):
+            pass_a(0, r, False)
+            pass_a(1, r, True)
         for r in range(PACK):
             nc.scalar.activation(out=y_a[:, r, :], in_=acc_a[r][:], func=SILU)
             nc.sync.dma_start(out=out_rows[:, r, 0:TB], in_=y_a[:, r, :])
         for r in range(PACK):
             pass_c(acc_b, TB, r, True, False)
 
-        interleave(vcopy, xb_bf[0, 0], xb_raw[0, 0], 0, HALF)
-        quantize_xb(0, 0)
-        interleave(vcopy, xb_bf[0, 1], xb_raw[0, 1], 0, HALF)
-        deal_scales(wb_s, wb_s_raw)
-        quantize_xb(0, 1)
+        for g in range(2):
+            for h in range(2):
+                interleave(vcopy, xb_bf[g, h], xb_raw[g, h], 0, HALF)
+            for h in range(2):
+                quantize_xb(g, h)
         for r in range(PACK):
             pass_b(0, r, False)
-        interleave(vcopy, xb_bf[1, 0], xb_raw[1, 0], 0, HALF)
-        interleave(scopy, xb_bf[1, 1], xb_raw[1, 1], 160, HALF)
-        interleave(vcopy, xb_bf[1, 1], xb_raw[1, 1], 0, 160)
-        quantize_xb(1, 0)
-        quantize_xb(1, 1)
-        for r in range(PACK):
             pass_b(1, r, True)
 
         interleave(scopy, ya_bf, y_a, 0, 128)
         interleave(vcopy, ya_bf, y_a, 128, TB)
         quantize(words_a[:], y_s[:, 0:TB], ya_bf)
 
-        for r in range(2):
-            nc.scalar.activation(
-                out=y_b[:, :, r, :], in_=acc_b[r][:].rearrange("p (h c) -> p h c", h=2), func=SILU
-            )
+        for r in range(PACK):
+            if r < PACK - 1:
+                nc.scalar.activation(
+                    out=y_b[:, :, r, :], in_=acc_b[r][:].rearrange("p (h c) -> p h c", h=2), func=SILU
+                )
+            else:
+                silu_b(r, 0)
+                interleave(vcopy, yb_bf[0], y_b[:, 0], 0, HALF)
+                silu_b(r, 1)
             nc.sync.dma_start(
                 out=out_rows[:, r, TB : 2 * TB].rearrange("p (h c) -> p h c", h=2), in_=y_b[:, :, r, :]
             )
-        store_words(words_a, 0, TB)
-        for h in range(2):
-            silu_b(2, h)
-            silu_b(3, h)
-            t0 = TB + HALF * h
-            nc.sync.dma_start(out=out_rows[:, 2:4, t0 : t0 + HALF], in_=y_b[:, h, 2:4, :])
-            if h == 0:
-                interleave(vcopy, yb_bf[0], y_b[:, 0], 0, HALF)
-        interleave(scopy, yb_bf[1], y_b[:, 1], 160, HALF)
-        interleave(vcopy, yb_bf[1], y_b[:, 1], 0, 160)
+            if r == 1:
+                store_words(words_a, 0, TB)
+        interleave(scopy, yb_bf[1], y_b[:, 1], 128, HALF)
+        interleave(vcopy, yb_bf[1], y_b[:, 1], 0, 128)
         for h in range(2):
             t0 = TB + HALF * h
             quantize(words_b[h][:], y_s[:, t0 : t0 + HALF], yb_bf[h])

@@ -34,7 +34,7 @@ def tile_mix_two_batches_one_context_pl_kernel(
 
         wa_raw = tile("wa_raw", [P, 2, NF], I32)
         wa = [tile("wa%d" % z, [P, NF], I32) for z in range(2)]
-        staged = tile("staged", [16, 9 * NF], U8)
+        staged = tile("staged", [32, 9 * NF], U8)
         planes = tile("planes", [P, 9 * NF], U8)
 
         def plane(first, passes, width):
@@ -53,15 +53,15 @@ def tile_mix_two_batches_one_context_pl_kernel(
         wc = tile("wc", [P, 1, 2 * NF], U8)
         wc_s = tile("wc_s", [P, 1, NF], U8)
         xa = tile("xa", [P, 2, 2 * TB], U8)
-        cx = tile("cx", [P, 2 * TB], I32)
-        xb_raw = {(g, h): tile("xb_raw%d%d" % (g, h), [P, PACK, HALF], F32) for g in range(2) for h in range(2)}
-        xb_bf = {(g, h): tile("xb_bf%d%d" % (g, h), [P, HALF, PACK], BF16) for g in range(2) for h in range(2)}
+        cx = [tile("cx%d" % b, [P, TB], I32) for b in range(2)]
+        xb_raw = [tile("xb_raw%d" % g, [P, PACK, TB], F32) for g in range(2)]
+        xb_bf = [tile("xb_bf%d" % g, [P, TB, PACK], BF16) for g in range(2)]
         xq = [tile("xq%d" % g, [P, TB], U32) for g in range(2)]
         xq_s = [tile("xq_s%d" % g, [P, TB], U8) for g in range(2)]
         y_a = tile("y_a", [P, PACK, TB], F32)
-        y_b = tile("y_b", [P, 2, PACK, HALF], F32)
+        y_b = tile("y_b", [P, PACK, TB], F32)
         ya_bf = tile("ya_bf", [P, TB, PACK], BF16)
-        yb_bf = [tile("yb_bf%d" % h, [P, HALF, PACK], BF16) for h in range(2)]
+        yb_bf = tile("yb_bf", [P, TB, PACK], BF16)
         words_a = tile("words_a", [P, TB], U32)
         words_b = [tile("words_b%d" % h, [P, HALF], U32) for h in range(2)]
         y_s = tile("y_s", [P, 2 * TB], U8)
@@ -73,18 +73,19 @@ def tile_mix_two_batches_one_context_pl_kernel(
 
         def stage_scales(queue, first, dram):
             passes, rows, width = dram.shape
-            dst = staged[:, first * NF : first * NF + passes * width].rearrange("q (z c) -> q z c", z=passes)
+            dst = staged[16:32, first * NF : first * NF + passes * width].rearrange("q (z c) -> q z c", z=passes)
             queue.dma_start(out=dst.bitcast(I32), in_=dram.rearrange("z q c -> q z c").bitcast(I32))
 
         def load_fp4(dst, dram):
             nc.sync.dma_start(out=dst[:].bitcast(I32), in_=dram.rearrange("z p c -> p z c").bitcast(I32))
 
-        def load_fp8(dst, dram):
-            nc.sync.dma_start(out=dst[:], in_=dram.rearrange("p c i -> p (c i)").bitcast(I32))
+        def load_cx(batch):
+            cols = cx_words[0, :, TB * batch : TB * (batch + 1), :]
+            nc.sync.dma_start(out=cx[batch][:], in_=cols.rearrange("p c i -> p (c i)").bitcast(I32))
 
-        def load_xb(g, h):
-            rows = xb[512 * g : 512 * (g + 1), HALF * h : HALF * (h + 1)]
-            nc.sync.dma_start(out=xb_raw[g, h][:], in_=rows.rearrange("(p j) u -> p j u", j=PACK))
+        def load_xb(g):
+            rows = xb[512 * g : 512 * (g + 1), :]
+            nc.sync.dma_start(out=xb_raw[g][:], in_=rows.rearrange("(p j) u -> p j u", j=PACK))
 
         def deal_fp8(z):
             nc.vector.tensor_copy(
@@ -111,11 +112,11 @@ def tile_mix_two_batches_one_context_pl_kernel(
             )
 
         def quantize(words, scales, src):
-            nc.vector.quantize_mx(out=words.bitcast(FP8X4), scales=scales, in_=src[:].rearrange("p c j -> p (c j)"))
+            nc.vector.quantize_mx(out=words.bitcast(FP8X4), scales=scales, in_=src.rearrange("p c j -> p (c j)"))
 
         def quantize_xb(g, h):
             cols = slice(HALF * h, HALF * (h + 1))
-            quantize(xq[g][:, cols], xq_s[g][:, cols], xb_bf[g, h])
+            quantize(xq[g][:, cols], xq_s[g][:, cols], xb_bf[g][:, cols, :])
 
         def fp4_cols(w, z, r):
             return w[:, z, 2 * P * r : 2 * P * (r + 1)].bitcast(FP4X4)
@@ -127,20 +128,20 @@ def tile_mix_two_batches_one_context_pl_kernel(
                 rhs=xa[:, z, :].bitcast(FP4X4), rhs_scale=xa_s[:, z, :], start=False, stop=stop,
             )
 
-        def pass_b(g, r, stop):
+        def pass_b(g, r):
             nc.tensor.matmul_mx(
                 out=acc_b[r][:], lhsT=fp4_cols(wb, g, r), lhsT_scale=wb_s[:, g, P * r : P * (r + 1)],
-                rhs=xq[g][:].bitcast(FP8X4), rhs_scale=xq_s[g][:], start=False, stop=stop,
+                rhs=xq[g][:].bitcast(FP8X4), rhs_scale=xq_s[g][:], start=(g == 0), stop=(g == 1),
             )
 
         def pass_c(acc, t0, r, start, stop):
             nc.tensor.matmul_mx(
                 out=acc[r][:], lhsT=fp4_cols(wc, 0, r), lhsT_scale=wc_s[:, 0, P * r : P * (r + 1)],
-                rhs=cx[:, t0 : t0 + TB].bitcast(FP8X4), rhs_scale=cx_s[:, 0, t0 : t0 + TB], start=start, stop=stop,
+                rhs=cx[t0 // TB][:].bitcast(FP8X4), rhs_scale=cx_s[:, 0, t0 : t0 + TB], start=start, stop=stop,
             )
 
         def silu_b(r, h):
-            nc.scalar.activation(out=y_b[:, h, r, :], in_=acc_b[r][:, HALF * h : HALF * (h + 1)], func=SILU)
+            nc.scalar.activation(out=y_b[:, r, HALF * h : HALF * (h + 1)], in_=acc_b[r][:, HALF * h : HALF * (h + 1)], func=SILU)
 
         def store_words(src, t0, width):
             nc.sync.dma_start(out=out_words[:, t0 : t0 + width], in_=src[:].bitcast(I32))
@@ -155,24 +156,22 @@ def tile_mix_two_batches_one_context_pl_kernel(
         stage_scales(nc.scalar, 5, xa_scales)
         stage_scales(nc.sync, 7, wb_scales)
         load_fp4(wc_raw, wc_words)
-        load_fp8(cx, cx_words[0])
+        load_cx(0)
         nc.sync.dma_start(out=wa_raw[:], in_=wa_words.rearrange("z p c i -> p z (c i)").bitcast(I32))
-        for q in range(4):
-            nc.sync.dma_start(
-                out=planes[32 * q : 32 * q + 4, :].bitcast(I32), in_=staged[4 * q : 4 * q + 4, :].bitcast(I32)
-            )
-        load_fp4(wb_raw, wb_words)
+        for i in range(4):
+            nc.sync.dma_start(out=planes[i:P:32, :].bitcast(I32), in_=staged[16 + i : 32 : 4, :].bitcast(I32))
         load_fp4(xa, xa_words)
-        for g in range(2):
-            for h in range(2):
-                load_xb(g, h)
+        load_fp4(wb_raw, wb_words)
+        load_xb(0)
+        load_xb(1)
+        load_cx(1)
 
         deal_fp4(wc, wc_raw, 0)
         deal_fp8(0)
         deal_fp8(1)
-        deal_fp4(wb, wb_raw, 0)
         deal_scales(wc_s, wc_s_raw)
         deal_scales(wa_s, wa_s_raw)
+        deal_fp4(wb, wb_raw, 0)
         deal_fp4(wb, wb_raw, 1)
         deal_scales(wb_s, wb_s_raw)
 
@@ -184,44 +183,41 @@ def tile_mix_two_batches_one_context_pl_kernel(
         for r in range(PACK):
             nc.scalar.activation(out=y_a[:, r, :], in_=acc_a[r][:], func=SILU)
             nc.sync.dma_start(out=out_rows[:, r, 0:TB], in_=y_a[:, r, :])
-        for r in range(PACK):
-            pass_c(acc_b, TB, r, True, False)
 
-        for g in range(2):
-            for h in range(2):
-                interleave(vcopy, xb_bf[g, h], xb_raw[g, h], 0, HALF)
-            for h in range(2):
-                quantize_xb(g, h)
+        for h in range(2):
+            interleave(vcopy, xb_bf[0], xb_raw[0], HALF * h, HALF * (h + 1))
+        for h in range(2):
+            quantize_xb(0, h)
         for r in range(PACK):
-            pass_b(0, r, False)
-            pass_b(1, r, True)
+            pass_b(0, r)
+        interleave(scopy, xb_bf[1], xb_raw[1], 368, TB)
+        interleave(vcopy, xb_bf[1], xb_raw[1], 0, HALF)
+        interleave(vcopy, xb_bf[1], xb_raw[1], HALF, 368)
+        for h in range(2):
+            quantize_xb(1, h)
+        for r in range(PACK):
+            pass_c(acc_b, TB, r, False, False)
+            pass_b(1, r)
 
-        interleave(scopy, ya_bf, y_a, 0, 128)
-        interleave(vcopy, ya_bf, y_a, 128, TB)
-        quantize(words_a[:], y_s[:, 0:TB], ya_bf)
+        interleave(vcopy, ya_bf, y_a, 0, TB)
+        quantize(words_a[:], y_s[:, 0:TB], ya_bf[:])
 
         for r in range(PACK):
             if r < PACK - 1:
-                nc.scalar.activation(
-                    out=y_b[:, :, r, :], in_=acc_b[r][:].rearrange("p (h c) -> p h c", h=2), func=SILU
-                )
+                nc.scalar.activation(out=y_b[:, r, :], in_=acc_b[r][:], func=SILU)
             else:
                 silu_b(r, 0)
-                interleave(vcopy, yb_bf[0], y_b[:, 0], 0, HALF)
                 silu_b(r, 1)
-            nc.sync.dma_start(
-                out=out_rows[:, r, TB : 2 * TB].rearrange("p (h c) -> p h c", h=2), in_=y_b[:, :, r, :]
-            )
+            nc.sync.dma_start(out=out_rows[:, r, TB : 2 * TB], in_=y_b[:, r, :])
             if r == 1:
                 store_words(words_a, 0, TB)
-        interleave(scopy, yb_bf[1], y_b[:, 1], 128, HALF)
-        interleave(vcopy, yb_bf[1], y_b[:, 1], 0, 128)
+        interleave(scopy, yb_bf, y_b, 384, TB)
+        interleave(vcopy, yb_bf, y_b, 0, HALF)
+        interleave(vcopy, yb_bf, y_b, HALF, 384)
         for h in range(2):
             t0 = TB + HALF * h
-            quantize(words_b[h][:], y_s[:, t0 : t0 + HALF], yb_bf[h])
+            quantize(words_b[h][:], y_s[:, t0 : t0 + HALF], yb_bf[:, HALF * h : HALF * (h + 1), :])
             store_words(words_b[h], t0, HALF)
-        for q in range(4):
-            eng = nc.sync if q < 2 else nc.scalar
-            eng.dma_start(
-                out=out_2[0, 4 * q : 4 * q + 4, :].bitcast(I32), in_=y_s[32 * q : 32 * q + 4, :].bitcast(I32)
-            )
+        for i in range(4):
+            eng = nc.sync if i < 2 else nc.scalar
+            eng.dma_start(out=out_2[0, i:16:4, :].bitcast(I32), in_=y_s[i:P:32, :].bitcast(I32))

@@ -54,7 +54,8 @@ def tile_mix_two_batches_one_context_pl_kernel(
         wc_s = tile("wc_s", [P, 1, NF], U8)
         xa = tile("xa", [P, 2, 2 * TB], U8)
         cx = [tile("cx%d" % b, [P, TB], I32) for b in range(2)]
-        xb_raw = [tile("xb_raw%d" % g, [P, PACK, TB], F32) for g in range(2)]
+        xb_raw0 = tile("xb_raw0", [P, PACK, TB], F32)
+        xb_raw1 = [tile("xb_raw1%d" % h, [P, PACK, HALF], F32) for h in range(2)]
         xb_bf = [tile("xb_bf%d" % g, [P, TB, PACK], BF16) for g in range(2)]
         xq = [tile("xq%d" % g, [P, TB], U32) for g in range(2)]
         xq_s = [tile("xq_s%d" % g, [P, TB], U8) for g in range(2)]
@@ -83,9 +84,9 @@ def tile_mix_two_batches_one_context_pl_kernel(
             cols = cx_words[0, :, TB * batch : TB * (batch + 1), :]
             nc.sync.dma_start(out=cx[batch][:], in_=cols.rearrange("p c i -> p (c i)").bitcast(I32))
 
-        def load_xb(g):
-            rows = xb[512 * g : 512 * (g + 1), :]
-            nc.sync.dma_start(out=xb_raw[g][:], in_=rows.rearrange("(p j) u -> p j u", j=PACK))
+        def load_xb(dst, g, c0, c1):
+            rows = xb[512 * g : 512 * (g + 1), c0:c1]
+            nc.sync.dma_start(out=dst[:], in_=rows.rearrange("(p j) u -> p j u", j=PACK))
 
         def deal_fp8(z):
             nc.vector.tensor_copy(
@@ -162,8 +163,9 @@ def tile_mix_two_batches_one_context_pl_kernel(
             nc.sync.dma_start(out=planes[i:P:32, :].bitcast(I32), in_=staged[16 + i : 32 : 4, :].bitcast(I32))
         load_fp4(xa, xa_words)
         load_fp4(wb_raw, wb_words)
-        load_xb(0)
-        load_xb(1)
+        load_xb(xb_raw0, 0, 0, TB)
+        for h in range(2):
+            load_xb(xb_raw1[h], 1, HALF * h, HALF * (h + 1))
         load_cx(1)
 
         deal_fp4(wc, wc_raw, 0)
@@ -185,21 +187,21 @@ def tile_mix_two_batches_one_context_pl_kernel(
             nc.sync.dma_start(out=out_rows[:, r, 0:TB], in_=y_a[:, r, :])
 
         for h in range(2):
-            interleave(vcopy, xb_bf[0], xb_raw[0], HALF * h, HALF * (h + 1))
+            interleave(vcopy, xb_bf[0], xb_raw0, HALF * h, HALF * (h + 1))
         for h in range(2):
             quantize_xb(0, h)
         for r in range(PACK):
             pass_b(0, r)
-        interleave(scopy, xb_bf[1], xb_raw[1], 368, TB)
-        interleave(vcopy, xb_bf[1], xb_raw[1], 0, HALF)
-        interleave(vcopy, xb_bf[1], xb_raw[1], HALF, 368)
+        for h in range(2):
+            interleave(vcopy, xb_bf[1][:, HALF * h : HALF * (h + 1), :], xb_raw1[h], 0, HALF)
         for h in range(2):
             quantize_xb(1, h)
         for r in range(PACK):
             pass_c(acc_b, TB, r, False, False)
             pass_b(1, r)
 
-        interleave(vcopy, ya_bf, y_a, 0, TB)
+        interleave(scopy, ya_bf, y_a, 0, 128)
+        interleave(vcopy, ya_bf, y_a, 128, TB)
         quantize(words_a[:], y_s[:, 0:TB], ya_bf[:])
 
         for r in range(PACK):

from contextlib import ExitStack

import concourse.mybir as mybir

F32 = mybir.dt.float32
BF16 = mybir.dt.bfloat16
I32 = mybir.dt.int32
U32 = mybir.dt.uint32
U8 = mybir.dt.uint8
FP8X4 = mybir.dt.float8_e4m3fn_x4
FP4X4 = mybir.dt.float4_e2m1fn_x4
SILU = mybir.ActivationFunctionType.Silu

P = 128
PACK = 4
NF = 512
TB = 512
HALF = 256
FLOPS = 3 * 2 * 1024 * 512 * 512


def tile_mix_two_batches_one_context_pl_kernel(
    tc, xa_words, xa_scales, wa_words, wa_scales, xb, wb_words, wb_scales,
    cx_words, cx_scales, wc_words, wc_scales, out_0, out_1, out_2,
):
    nc = tc.nc
    with ExitStack() as ctx:
        sb = ctx.enter_context(tc.tile_pool(name="sb", bufs=1))
        ps = ctx.enter_context(tc.psum_pool(name="ps", bufs=1))
        ctx.enter_context(tc.manual_schedule())

        def tile(name, shape, dtype):
            return sb.tile(shape, dtype, name=name, align_bytes=64)

        wa_raw = tile("wa_raw", [P, 2, NF], I32)
        wa = [tile("wa%d" % z, [P, NF], I32) for z in range(2)]
        staged = tile("staged", [32, 9 * NF], U8)
        planes = tile("planes", [P, 9 * NF], U8)

        def plane(first, passes, width):
            return planes[:, first * NF : first * NF + passes * width].rearrange("p (z c) -> p z c", z=passes)

        wc_s_raw = plane(0, 1, NF)
        cx_s = plane(1, 1, 2 * TB)
        wa_s_raw = plane(3, 2, NF)
        xa_s = plane(5, 2, TB)
        wb_s_raw = plane(7, 2, NF)
        wa_s = tile("wa_s", [P, 2, NF], U8)
        wb_raw = tile("wb_raw", [P, 2, 2 * NF], U8)
        wb = tile("wb", [P, 2, 2 * NF], U8)
        wb_s = tile("wb_s", [P, 2, NF], U8)
        wc_raw = tile("wc_raw", [P, 1, 2 * NF], U8)
        wc = tile("wc", [P, 1, 2 * NF], U8)
        wc_s = tile("wc_s", [P, 1, NF], U8)
        xa = tile("xa", [P, 2, 2 * TB], U8)
        cx = [tile("cx%d" % b, [P, TB], I32) for b in range(2)]
        xb_raw0 = tile("xb_raw0", [P, PACK, TB], F32)
        xb_raw1 = [tile("xb_raw1%d" % h, [P, PACK, HALF], F32) for h in range(2)]
        xb_bf = [tile("xb_bf%d" % g, [P, TB, PACK], BF16) for g in range(2)]
        xq = [tile("xq%d" % g, [P, TB], U32) for g in range(2)]
        xq_s = [tile("xq_s%d" % g, [P, TB], U8) for g in range(2)]
        y_a = tile("y_a", [P, PACK, TB], F32)
        y_b = tile("y_b", [P, PACK, TB], F32)
        ya_bf = tile("ya_bf", [P, TB, PACK], BF16)
        yb_bf = tile("yb_bf", [P, TB, PACK], BF16)
        words_a = tile("words_a", [P, TB], U32)
        words_b = [tile("words_b%d" % h, [P, HALF], U32) for h in range(2)]
        y_s = tile("y_s", [P, 2 * TB], U8)
        acc_a = [ps.tile([P, TB], F32, name="acc_a%d" % r) for r in range(PACK)]
        acc_b = [ps.tile([P, TB], F32, name="acc_b%d" % r) for r in range(PACK)]

        out_rows = out_0.rearrange("(p r) t -> p r t", r=PACK)
        out_words = out_1[0].rearrange("p t i -> p (t i)").bitcast(I32)

        def stage_scales(queue, first, dram):
            passes, rows, width = dram.shape
            dst = staged[16:32, first * NF : first * NF + passes * width].rearrange("q (z c) -> q z c", z=passes)
            queue.dma_start(out=dst.bitcast(I32), in_=dram.rearrange("z q c -> q z c").bitcast(I32))

        def load_fp4(dst, dram):
            nc.sync.dma_start(out=dst[:].bitcast(I32), in_=dram.rearrange("z p c -> p z c").bitcast(I32))

        def load_cx(batch):
            cols = cx_words[0, :, TB * batch : TB * (batch + 1), :]
            nc.sync.dma_start(out=cx[batch][:], in_=cols.rearrange("p c i -> p (c i)").bitcast(I32))

        def load_xb(dst, g, c0, c1):
            rows = xb[512 * g : 512 * (g + 1), c0:c1]
            nc.sync.dma_start(out=dst[:], in_=rows.rearrange("(p j) u -> p j u", j=PACK))

        def deal_fp8(z):
            nc.vector.tensor_copy(
                out=wa[z][:].rearrange("p (r a b) -> p a r b", r=PACK, b=4),
                in_=wa_raw[:, z, :].rearrange("p (a b r) -> p a r b", r=PACK, b=4),
            )

        def deal_fp4(dst, raw, z):
            nc.vector.tensor_copy(
                out=dst[:, z, :].rearrange("p (r m b) -> p r m b", r=PACK, b=2),
                in_=raw[:, z, :].rearrange("p (m r b) -> p r m b", r=PACK, b=2),
            )

        def deal_scales(dst, raw):
            nc.vector.tensor_copy(
                out=dst[:].rearrange("p z (r m) -> p z r m", r=PACK),
                in_=raw.rearrange("p z (m r) -> p z r m", r=PACK),
            )

        def interleave(copy, dst, src, c0, c1):
            copy(
                out=dst[:, c0:c1, :].rearrange("p (c i) j -> p c j i", i=4),
                in_=src[:, :, c0:c1].rearrange("p j (c i) -> p c j i", i=4),
            )

        def quantize(words, scales, src):
            nc.vector.quantize_mx(out=words.bitcast(FP8X4), scales=scales, in_=src.rearrange("p c j -> p (c j)"))

        def quantize_xb(g, h):
            cols = slice(HALF * h, HALF * (h + 1))
            quantize(xq[g][:, cols], xq_s[g][:, cols], xb_bf[g][:, cols, :])

        def fp4_cols(w, z, r):
            return w[:, z, 2 * P * r : 2 * P * (r + 1)].bitcast(FP4X4)

        def pass_a(z, r, stop):
            nc.tensor.matmul_mx(
                out=acc_a[r][:], lhsT=wa[z][:, P * r : P * (r + 1)].bitcast(FP8X4),
                lhsT_scale=wa_s[:, z, P * r : P * (r + 1)],
                rhs=xa[:, z, :].bitcast(FP4X4), rhs_scale=xa_s[:, z, :], start=False, stop=stop,
            )

        def pass_b(g, r):
            nc.tensor.matmul_mx(
                out=acc_b[r][:], lhsT=fp4_cols(wb, g, r), lhsT_scale=wb_s[:, g, P * r : P * (r + 1)],
                rhs=xq[g][:].bitcast(FP8X4), rhs_scale=xq_s[g][:], start=(g == 0), stop=(g == 1),
            )

        def pass_c(acc, t0, r, start, stop):
            nc.tensor.matmul_mx(
                out=acc[r][:], lhsT=fp4_cols(wc, 0, r), lhsT_scale=wc_s[:, 0, P * r : P * (r + 1)],
                rhs=cx[t0 // TB][:].bitcast(FP8X4), rhs_scale=cx_s[:, 0, t0 : t0 + TB], start=start, stop=stop,
            )

        def silu_b(r, h):
            nc.scalar.activation(out=y_b[:, r, HALF * h : HALF * (h + 1)], in_=acc_b[r][:, HALF * h : HALF * (h + 1)], func=SILU)

        def store_words(src, t0, width):
            nc.sync.dma_start(out=out_words[:, t0 : t0 + width], in_=src[:].bitcast(I32))

        vcopy = nc.vector.tensor_copy
        scopy = nc.scalar.copy

        nc.vector.memset(planes[:].bitcast(U32), 0)
        stage_scales(nc.sync, 0, wc_scales)
        stage_scales(nc.scalar, 1, cx_scales)
        stage_scales(nc.sync, 3, wa_scales)
        stage_scales(nc.scalar, 5, xa_scales)
        stage_scales(nc.sync, 7, wb_scales)
        load_fp4(wc_raw, wc_words)
        load_cx(0)
        nc.sync.dma_start(out=wa_raw[:], in_=wa_words.rearrange("z p c i -> p z (c i)").bitcast(I32))
        for i in range(4):
            nc.sync.dma_start(out=planes[i:P:32, :].bitcast(I32), in_=staged[16 + i : 32 : 4, :].bitcast(I32))
        load_fp4(xa, xa_words)
        load_fp4(wb_raw, wb_words)
        load_xb(xb_raw0, 0, 0, TB)
        for h in range(2):
            load_xb(xb_raw1[h], 1, HALF * h, HALF * (h + 1))
        load_cx(1)

        deal_fp4(wc, wc_raw, 0)
        deal_fp8(0)
        deal_fp8(1)
        deal_scales(wc_s, wc_s_raw)
        deal_scales(wa_s, wa_s_raw)
        deal_fp4(wb, wb_raw, 0)
        deal_fp4(wb, wb_raw, 1)
        deal_scales(wb_s, wb_s_raw)

        for r in range(PACK):
            pass_c(acc_a, 0, r, True, False)
        for r in range(PACK):
            pass_a(0, r, False)
            pass_a(1, r, True)
        for r in range(PACK):
            nc.scalar.activation(out=y_a[:, r, :], in_=acc_a[r][:], func=SILU)
            nc.sync.dma_start(out=out_rows[:, r, 0:TB], in_=y_a[:, r, :])

        for h in range(2):
            interleave(vcopy, xb_bf[0], xb_raw0, HALF * h, HALF * (h + 1))
        for h in range(2):
            quantize_xb(0, h)
        for r in range(PACK):
            pass_b(0, r)
        for h in range(2):
            interleave(vcopy, xb_bf[1][:, HALF * h : HALF * (h + 1), :], xb_raw1[h], 0, HALF)
        for h in range(2):
            quantize_xb(1, h)
        for r in range(PACK):
            pass_c(acc_b, TB, r, False, False)
            pass_b(1, r)

        interleave(scopy, ya_bf, y_a, 0, 128)
        interleave(vcopy, ya_bf, y_a, 128, TB)
        quantize(words_a[:], y_s[:, 0:TB], ya_bf[:])

        for r in range(PACK):
            if r < PACK - 1:
                nc.scalar.activation(out=y_b[:, r, :], in_=acc_b[r][:], func=SILU)
            else:
                silu_b(r, 0)
                silu_b(r, 1)
            nc.sync.dma_start(out=out_rows[:, r, TB : 2 * TB], in_=y_b[:, r, :])
            if r == 1:
                store_words(words_a, 0, TB)
        interleave(scopy, yb_bf, y_b, 384, TB)
        interleave(vcopy, yb_bf, y_b, 0, HALF)
        interleave(vcopy, yb_bf, y_b, HALF, 384)
        for h in range(2):
            t0 = TB + HALF * h
            quantize(words_b[h][:], y_s[:, t0 : t0 + HALF], yb_bf[:, HALF * h : HALF * (h + 1), :])
            store_words(words_b[h], t0, HALF)
        for i in range(4):
            eng = nc.sync if i < 2 else nc.scalar
            eng.dma_start(out=out_2[0, i:16:4, :].bitcast(I32), in_=y_s[i:P:32, :].bitcast(I32))
